import numpy as np
import ml_dtypes


def mxq(x, axis, fmt="e4m3"):
    dtype, down = {"e4m3": (ml_dtypes.float8_e4m3fn, 7), "e5m2": (ml_dtypes.float8_e5m2, 14)}[fmt]
    v = np.moveaxis(np.asarray(x, np.float32).astype(ml_dtypes.bfloat16).astype(np.float64), axis, -1)
    blocks = v.reshape(v.shape[:-1] + (-1, 32))
    amax = np.abs(blocks).max(-1, keepdims=True)
    byte = np.maximum(np.where(amax > 0, np.frexp(amax)[1] - 1 + 127, 0) - down, 1)
    scale = np.exp2(byte - 127.0)
    codes = (blocks / scale).astype(np.float32).astype(dtype).astype(np.float64)
    return np.moveaxis((codes * scale).reshape(v.shape), -1, axis)


WIDE = False


def mx_kscale(k):
    if not WIDE:
        return np.ones(k)
    levels = np.array([10, -10, 5, -5, 0])
    if k % 512:
        return np.exp2(np.random.permutation(np.resize(levels, k // 32))).repeat(32)
    a = np.empty((k // 512, 16))
    for p in range(k // 512):
        a[p, :8] = np.random.permutation(np.resize(levels, 8))
        for g in range(8):
            far = levels[np.abs(levels - a[p, g]) >= 10]
            a[p, g + 8] = far[np.random.randint(len(far))]
    return np.exp2(a.ravel()).repeat(32)


def f64(x):
    return np.asarray(x).astype(np.float64)


def striped(idx):
    return np.tile(np.asarray(idx).reshape(-1, 16).T, (8, 1)).astype(np.uint16)


def unstriped(offs):
    return offs[:16].T.reshape(-1).astype(np.int64)


E2M1 = np.array([0.0, 0.5, 1.0, 1.5, 2.0, 3.0, 4.0, 6.0, -0.0, -0.5, -1.0, -1.5, -2.0, -3.0, -4.0, -6.0])


def pack_weight(w, fmt):
    k, n = w.shape
    w = f64(np.asarray(w, np.float32).astype(ml_dtypes.bfloat16)).reshape(k // 32, 32, n)
    amax = np.abs(w).max(1)
    if fmt == "e4m3":
        byte = np.frexp(amax)[1] - 1 + 127 - 7
    else:
        mant, ex = np.frexp(amax / 6.0)
        byte = np.where(mant > 0.5, ex, ex - 1) + 127
    byte = np.clip(np.where(amax > 0, byte, 1), 1, 254)
    scaled = (w * np.exp2(127.0 - byte)[:, None, :]).reshape(k, n).astype(np.float32)
    by_word = np.ascontiguousarray(scaled.reshape(k // 512, 128, 4, n).transpose(0, 1, 3, 2))
    if fmt == "e4m3":
        words = by_word.astype(ml_dtypes.float8_e4m3fn).view(np.uint8)
    else:
        c = by_word.astype(ml_dtypes.float4_e2m1fn).view(np.uint8) & 0xF
        words = (c[..., 0::2] | (c[..., 1::2] << 4)).reshape(k // 512, 128, 2 * n)
    return np.ascontiguousarray(words), np.ascontiguousarray(byte.astype(np.uint8).reshape(k // 512, 16, n))


def unpack_weight(words, scales, fmt):
    g, _, n = scales.shape
    words = np.ascontiguousarray(words).reshape(g, 128, n, -1)
    if fmt == "e4m3":
        vals = words.view(ml_dtypes.float8_e4m3fn).astype(np.float64)
    else:
        nib = np.empty((g, 128, n, 4), np.uint8)
        nib[..., 0::2] = words & 0xF
        nib[..., 1::2] = words >> 4
        vals = E2M1[nib]
    vals = vals * np.repeat(np.exp2(scales.astype(np.float64) - 127.0), 8, axis=1)[..., None]
    return vals.transpose(0, 1, 3, 2).reshape(g * 512, n)


def bf(x):
    return np.asarray(x, np.float32).astype(ml_dtypes.bfloat16)


def planes(Y):
    r, m = Y.shape
    b = f64(bf(Y)).reshape(r // 32, 32, m)
    amax = np.abs(b).max(1)
    byte = np.clip(np.where(amax > 0, np.frexp(amax)[1] - 1 + 127 - 7, 1), 1, 254)
    codes = (b * np.exp2(127.0 - byte)[:, None, :]).reshape(r, m).astype(np.float32).astype(ml_dtypes.float8_e4m3fn).view(np.uint8)
    words = codes.reshape(r // 512, 128, 4, m).transpose(0, 1, 3, 2)
    return np.ascontiguousarray(words), np.ascontiguousarray(byte.astype(np.uint8).reshape(r // 512, 16, m))


K, T, J, N = 1024, 1024, 512, 512


def setup_inputs():
    n = np.random.standard_normal
    idx = np.random.permutation(T)[:J]
    idx2 = np.random.permutation(T)[:J]
    idx3 = np.random.permutation(T)[:J]
    fk = mx_kscale(K)
    wp = pack_weight(n((K, N)) * 1 / np.sqrt(K) * fk[:, None], "e4m3")
    return {
        "xf": (n((K, T))).astype(np.float32),
        "fk": (np.random.uniform(0.5, 2.0, (K, 1)) / fk[:, None]).astype(np.float32),
        "w_words": wp[0],
        "w_scales": wp[1],
        "rw": (np.random.uniform(0.5, 2.0, (1, J))).astype(np.float32),
        "offs": striped(idx),
        "offs2": striped(idx2),
        "offs3": striped(idx3),
    }


def reference(xf, fk, w_words, w_scales, rw, offs, offs2, offs3):
    idx = unstriped(offs)
    idx2 = unstriped(offs2)
    idx3 = unstriped(offs3)
    wu = unpack_weight(w_words, w_scales, "e4m3")
    u = (np.maximum(f64(xf)[:, idx], np.maximum(f64(xf)[:, idx2], f64(xf)[:, idx3])) - 0.5 * f64(xf)[:, idx]) * f64(fk)
    uq = mxq(u, 0, "e4m3")
    p = wu.T @ uq
    y = p * f64(rw)
    words, scales = planes(y)
    return y, words, scales

@@ -1,0 +1,232 @@
+from contextlib import ExitStack
+
+import concourse.mybir as mybir
+from concourse.masks import make_identity
+
+K, T, J, N = 1024, 1024, 512, 512
+FLOPS = 2 * K * J * N
+
+F32 = mybir.dt.float32
+BF16 = mybir.dt.bfloat16
+I32 = mybir.dt.int32
+U32 = mybir.dt.uint32
+U16 = mybir.dt.uint16
+U8 = mybir.dt.uint8
+FP8X4 = mybir.dt.float8_e4m3fn_x4
+ALU = mybir.AluOpType
+COPY = mybir.ActivationFunctionType.Copy
+
+P = 128
+PACK = 4
+PASSES = K // (P * PACK)
+BLOCK = 128
+CHUNKS = (256, 128, 128)
+
+
+def tile_list_largest_of_three_lists_pl_kernel(tc, xf, fk, w_words, w_scales, rw, offs, offs2, offs3, out_0, out_1, out_2):
+    nc = tc.nc
+    with ExitStack() as ctx:
+        held = ctx.enter_context(tc.tile_pool(name="held", bufs=1))
+        ring = ctx.enter_context(tc.tile_pool(name="ring", bufs=2))
+        psum = ctx.enter_context(tc.psum_pool(name="psum", bufs=2))
+
+        lists = [held.tile([P, J // 16], U16, name="list%d" % i) for i in range(3)]
+        planes = [held.tile([P, T], F32, name="plane%d" % i) for i in range(PASSES * PACK)]
+        fk_sb = held.tile([P, PASSES, PACK], F32)
+        half_fk = held.tile([P, PASSES, PACK], F32)
+        rw_sb = held.tile([P, J // BLOCK], F32)
+        w_codes = held.tile([P, PASSES, N], U32, align_bytes=64)
+        w_plane = held.tile([P, PASSES, N], U8, align_bytes=64)
+        ident = held.tile([P, P], F32)
+        y_codes = held.tile([P, J], U32, align_bytes=64)
+        y_plane = held.tile([P, J], U8, align_bytes=64)
+
+        x_rows = xf.rearrange("(a p t) c -> a t p c", a=PASSES, t=PACK)
+
+        def load_plane(i):
+            nc.sync.dma_start(out=planes[i][:], in_=x_rows[i // PACK, i % PACK])
+
+        nc.gpsimd.memset(w_plane[:].rearrange("p a n -> p (a n)").bitcast(U32), 0)
+        make_identity(nc, ident[:])
+
+        nc.sync.dma_start(lists[0][:], offs)
+        load_plane(0)
+        nc.sync.dma_start(lists[1][:], offs2)
+        nc.sync.dma_start(lists[2][:], offs3)
+        nc.sync.dma_start(out=fk_sb[:], in_=fk.rearrange("(a p t) o -> p a (t o)", a=PASSES, t=PACK))
+        for i in range(1, PASSES * PACK):
+            load_plane(i)
+        nc.sync.dma_start(
+            out=w_codes[:].bitcast(I32),
+            in_=w_words.rearrange("a p n r -> p a (n r)").bitcast(I32),
+        )
+        for q in range(4):
+            nc.sync.dma_start(
+                out=w_plane[32 * q : 32 * q + 4].bitcast(I32),
+                in_=w_scales[:, 4 * q : 4 * q + 4, :].rearrange("a r n -> r a n").bitcast(I32),
+            )
+        with nc.allow_non_contiguous_dma(reason="one weight to a partition"):
+            nc.sync.dma_start(out=rw_sb[:], in_=rw.rearrange("o (b p) -> p (o b)", p=BLOCK))
+        nc.scalar.activation(out=half_fk[:], in_=fk_sb[:], func=COPY, scale=0.5)
+
+        y_rows = out_0.rearrange("(p t) j -> p t j", t=PACK)
+        words_out = out_1[0].rearrange("p j r -> p (j r)").bitcast(I32)
+
+        steps = []
+        j0 = 0
+        for n in CHUNKS:
+            for i in range(PASSES * PACK):
+                steps.append((j0, n, i))
+            j0 = j0 + n
+        last_group = (J - CHUNKS[-1], PASSES - 1)
+
+        pick = {}
+        diff = {}
+        sums = {}
+        flat = {}
+        quantised = {}
+        accs = {}
+
+        def window(step, which):
+            j0, n, i = step
+            return planes[i][:].indirect(lists[which][:, j0 // 16 : (j0 + n) // 16])
+
+        def gather_first(step):
+            pick[step] = ring.tile([P, 2, step[1]], F32, name="pick", bufs=4)
+            nc.vector.tensor_copy(pick[step][:, 0, :], window(step, 0))
+
+        def gather_others(step):
+            diff[step] = ring.tile([P, 2, step[1]], F32, name="diff", bufs=3)
+            for which in (1, 2):
+                nc.vector.tensor_tensor(diff[step][:, which - 1, :], window(step, which), pick[step][:, 0, :], ALU.subtract)
+
+        def largest(step):
+            j0, n, i = step
+            a, t = divmod(i, PACK)
+            nc.vector.scalar_tensor_tensor(
+                out=pick[step][:, 1, :], in0=diff[step][:, 0, :], scalar=0.0, in1=diff[step][:, 1, :], op0=ALU.max, op1=ALU.max
+            )
+            if (j0, a) == last_group:
+                share = ring.tile([P, n], F32, name="share", bufs=4)
+                nc.scalar.activation(out=share[:], in_=pick[step][:, 0, :], func=COPY, scale=half_fk[:, a, t : t + 1])
+                if t == 0:
+                    flat[j0, a] = held.tile([P, PACK, n], BF16, name="flat")
+                sums[step] = share
+                return
+            scaled = ring.tile([P, 2, n], F32, name="scaled", bufs=3)
+            nc.scalar.activation(out=scaled[:], in_=pick[step][:], func=COPY, scale=half_fk[:, a, t : t + 1])
+            for b in range(n // BLOCK):
+                if t == 0:
+                    sums[j0, a, b] = psum.tile([P, PACK, P], F32, name="sums", bufs=3)
+                cols = slice(b * BLOCK, (b + 1) * BLOCK)
+                terms = (1, 1, 0)
+                for s, term in enumerate(terms):
+                    nc.tensor.matmul(
+                        sums[j0, a, b][:, t, :], lhsT=scaled[:, term, cols], rhs=ident[:], is_transpose=True,
+                        start=(s == 0), stop=(s == len(terms) - 1),
+                    )
+
+        def finish_on_vector(step):
+            j0, n, i = step
+            a, t = divmod(i, PACK)
+            nc.vector.scalar_tensor_tensor(
+                out=flat[j0, a][:, t, :], in0=pick[step][:, 1, :], scalar=fk_sb[:, a, t : t + 1], in1=sums[step][:],
+                op0=ALU.mult, op1=ALU.add,
+            )
+
+        def quantise(j0, n, a):
+            grouped = ring.tile([P, n * PACK], BF16, name="grouped", align_bytes=64)
+            if (j0, a) == last_group:
+                nc.vector.tensor_copy(
+                    out=grouped[:].rearrange("p (c i t) -> p c t i", i=4, t=PACK),
+                    in_=flat[j0, a][:].rearrange("p t (c i) -> p c t i", i=4),
+                )
+            else:
+                for b in range(n // BLOCK):
+                    rounded = ring.tile([P, PACK * P], BF16, name="rounded")
+                    nc.scalar.copy(
+                        out=rounded[:].rearrange("j (u p e) -> j u p e", u=2, e=2),
+                        in_=sums[j0, a, b][:].rearrange("j (u e) p -> j u p e", e=2),
+                    )
+                    pairs = psum.tile([P, 2, BLOCK], F32, name="pairs")
+                    words = rounded[:].bitcast(F32)
+                    for u in range(2):
+                        nc.tensor.transpose(pairs[:, u, :], words[:, u * P : (u + 1) * P], ident[:])
+                    nc.scalar.copy(
+                        out=grouped[:, b * BLOCK * PACK : (b + 1) * BLOCK * PACK].bitcast(F32).rearrange("p (j u) -> p j u", u=2),
+                        in_=pairs[:].rearrange("p u j -> p j u"),
+                    )
+            codes = ring.tile([P, n], U32, name="codes", bufs=3, align_bytes=64)
+            plane = ring.tile([P, n], U8, name="plane", bufs=3, align_bytes=64)
+            nc.vector.quantize_mx(out=codes[:].bitcast(FP8X4), scales=plane[:], in_=grouped[:])
+            quantised[j0, a] = (codes, plane)
+
+        def multiply(j0, b, a):
+            codes, plane = quantised[j0, a]
+            if a == 0:
+                accs[j0, b] = psum.tile([P, N], F32, name="acc")
+            cols = slice(b * BLOCK, (b + 1) * BLOCK)
+            nc.tensor.matmul_mx(
+                out=accs[j0, b][:], lhsT=codes[:, cols].bitcast(FP8X4), lhsT_scale=plane[:, cols],
+                rhs=w_codes[:, a, :].bitcast(FP8X4), rhs_scale=w_plane[:, a, :],
+                start=(a == 0), stop=(a == PASSES - 1),
+            )
+
+        def hand_out(j0, b):
+            jb = j0 // BLOCK + b
+            cols = slice(jb * BLOCK, (jb + 1) * BLOCK)
+            last = jb == J // BLOCK - 1
+            y_slots = ring.tile([P, PACK, P], F32, name="y_slots")
+            nc.scalar.activation(
+                out=y_slots[:], in_=accs[j0, b][:].rearrange("j (p t) -> j t p", t=PACK), func=COPY, scale=rw_sb[:, jb : jb + 1]
+            )
+            y_bank = psum.tile([P, PACK, BLOCK], F32, name="y_bank", bufs=1)
+            for t in range(PACK):
+                nc.tensor.transpose(y_bank[:, t, :], y_slots[:, t, :], ident[:])
+            y_grouped = ring.tile([P, BLOCK * PACK], BF16, name="y_grouped", align_bytes=64)
+            grouped_view = y_grouped[:].rearrange("p (j t) -> p j t", t=PACK)
+            bank_view = y_bank[:].rearrange("p t j -> p j t")
+            if last:
+                nc.vector.tensor_copy(out=grouped_view, in_=bank_view)
+            else:
+                nc.scalar.copy(out=grouped_view, in_=bank_view)
+            y_sb = ring.tile([P, PACK, BLOCK], F32, name="y_sb")
+            nc.scalar.copy(out=y_sb[:], in_=y_bank[:])
+            nc.sync.dma_start(out=y_rows[:, :, cols], in_=y_sb[:])
+            nc.vector.quantize_mx(out=y_codes[:, cols].bitcast(FP8X4), scales=y_plane[:, cols], in_=y_grouped[:])
+            nc.sync.dma_start(out=words_out[:, cols], in_=y_codes[:, cols].bitcast(I32))
+
+        def after(step):
+            j0, n, i = step
+            a, t = divmod(i, PACK)
+            if (j0, a) == last_group:
+                finish_on_vector(step)
+            if t != PACK - 1:
+                return
+            quantise(j0, n, a)
+            early = j0 > 0
+            for b in range(n // BLOCK):
+                if a == 0 and early:
+                    multiply(j0, b, 0)
+                if a == PASSES - 1:
+                    if not early:
+                        multiply(j0, b, 0)
+                    multiply(j0, b, 1)
+                    hand_out(j0, b)
+
+        gather_first(steps[0])
+        for s in range(len(steps) + 2):
+            if s + 1 < len(steps):
+                gather_first(steps[s + 1])
+            if s < len(steps):
+                gather_others(steps[s])
+            if 1 <= s <= len(steps):
+                largest(steps[s - 1])
+            if s >= 2:
+                after(steps[s - 2])
+
+        for q in range(4):
+            queue = nc.scalar if q % 2 else nc.sync
+            queue.dma_start(
+                out=out_2[0, 4 * q : 4 * q + 4, :].bitcast(I32), in_=y_plane[32 * q : 32 * q + 4, :].bitcast(I32)
+            )

@@ -20,7 +20,8 @@ P = 128
 PACK = 4
 PASSES = K // (P * PACK)
 BLOCK = 128
-CHUNKS = (256, 128, 128)
+GROUPS = ((0, 512, 0), (0, 256, 1), (256, 256, 1))
+BATCH = 2
 
 
 def tile_list_largest_of_three_lists_pl_kernel(tc, xf, fk, w_words, w_scales, rw, offs, offs2, offs3, out_0, out_1, out_2):
@@ -72,158 +73,177 @@ def tile_list_largest_of_three_lists_pl_kernel(tc, xf, fk, w_words, w_scales, rw
         y_rows = out_0.rearrange("(p t) j -> p t j", t=PACK)
         words_out = out_1[0].rearrange("p j r -> p (j r)").bitcast(I32)
 
-        steps = []
-        j0 = 0
-        for n in CHUNKS:
-            for i in range(PASSES * PACK):
-                steps.append((j0, n, i))
-            j0 = j0 + n
-        last_group = (J - CHUNKS[-1], PASSES - 1)
-
-        pick = {}
-        diff = {}
-        sums = {}
-        flat = {}
+        last_group = GROUPS[-1]
+        scaled = {}
+        batches = [(group, t0) for group in GROUPS for t0 in range(0, PACK, BATCH)]
+        pairs = {}
+        grouped = {}
         quantised = {}
-        accs = {}
 
-        def window(step, which):
-            j0, n, i = step
-            return planes[i][:].indirect(lists[which][:, j0 // 16 : (j0 + n) // 16])
+        def look_up(group, t0):
+            j0, n, a = group
 
-        def gather_first(step):
-            pick[step] = ring.tile([P, 2, step[1]], F32, name="pick", bufs=4)
-            nc.vector.tensor_copy(pick[step][:, 0, :], window(step, 0))
+            def window(t, which):
+                return planes[a * PACK + t][:].indirect(lists[which][:, j0 // 16 : (j0 + n) // 16])
 
-        def gather_others(step):
-            diff[step] = ring.tile([P, 2, step[1]], F32, name="diff", bufs=3)
-            for which in (1, 2):
-                nc.vector.tensor_tensor(diff[step][:, which - 1, :], window(step, which), pick[step][:, 0, :], ALU.subtract)
-
-        def largest(step):
-            j0, n, i = step
-            a, t = divmod(i, PACK)
-            nc.vector.scalar_tensor_tensor(
-                out=pick[step][:, 1, :], in0=diff[step][:, 0, :], scalar=0.0, in1=diff[step][:, 1, :], op0=ALU.max, op1=ALU.max
-            )
-            if (j0, a) == last_group:
-                share = ring.tile([P, n], F32, name="share", bufs=4)
-                nc.scalar.activation(out=share[:], in_=pick[step][:, 0, :], func=COPY, scale=half_fk[:, a, t : t + 1])
-                if t == 0:
-                    flat[j0, a] = held.tile([P, PACK, n], BF16, name="flat")
-                sums[step] = share
-                return
-            scaled = ring.tile([P, 2, n], F32, name="scaled", bufs=3)
-            nc.scalar.activation(out=scaled[:], in_=pick[step][:], func=COPY, scale=half_fk[:, a, t : t + 1])
-            for b in range(n // BLOCK):
-                if t == 0:
-                    sums[j0, a, b] = psum.tile([P, PACK, P], F32, name="sums", bufs=3)
-                cols = slice(b * BLOCK, (b + 1) * BLOCK)
-                terms = (1, 1, 0)
-                for s, term in enumerate(terms):
-                    nc.tensor.matmul(
-                        sums[j0, a, b][:, t, :], lhsT=scaled[:, term, cols], rhs=ident[:], is_transpose=True,
-                        start=(s == 0), stop=(s == len(terms) - 1),
-                    )
-
-        def finish_on_vector(step):
-            j0, n, i = step
-            a, t = divmod(i, PACK)
-            nc.vector.scalar_tensor_tensor(
-                out=flat[j0, a][:, t, :], in0=pick[step][:, 1, :], scalar=fk_sb[:, a, t : t + 1], in1=sums[step][:],
-                op0=ALU.mult, op1=ALU.add,
-            )
-
-        def quantise(j0, n, a):
-            grouped = ring.tile([P, n * PACK], BF16, name="grouped", align_bytes=64)
-            if (j0, a) == last_group:
-                nc.vector.tensor_copy(
-                    out=grouped[:].rearrange("p (c i t) -> p c t i", i=4, t=PACK),
-                    in_=flat[j0, a][:].rearrange("p t (c i) -> p c t i", i=4),
-                )
+            if (group, t0) == batches[-1]:
+                pick = held.tile([P, BATCH, 2, n], F32, name="hold%d_%d_%d" % GROUPS[-2], align_bytes=64)
             else:
-                for b in range(n // BLOCK):
-                    rounded = ring.tile([P, PACK * P], BF16, name="rounded")
-                    nc.scalar.copy(
-                        out=rounded[:].rearrange("j (u p e) -> j u p e", u=2, e=2),
-                        in_=sums[j0, a, b][:].rearrange("j (u e) p -> j u p e", e=2),
+                pick = ring.tile([P, BATCH, 2, n], F32, name="pick", bufs=2)
+            diff = ring.tile([P, BATCH, 2, n], F32, name="diff", bufs=2)
+            for s in range(BATCH):
+                nc.vector.tensor_copy(pick[:, s, 0, :], window(t0 + s, 0))
+            for s in range(BATCH):
+                for w in range(2):
+                    nc.vector.tensor_tensor(diff[:, s, w, :], window(t0 + s, w + 1), pick[:, s, 0, :], ALU.subtract)
+            for s in range(BATCH):
+                nc.vector.scalar_tensor_tensor(
+                    out=pick[:, s, 1, :], in0=diff[:, s, 0, :], scalar=0.0, in1=diff[:, s, 1, :], op0=ALU.max, op1=ALU.max
+                )
+            both = ring.tile([P, BATCH, 2, n], F32, name="both", bufs=3)
+            for s in range(BATCH):
+                t = t0 + s
+                nc.scalar.activation(out=both[:, s, 0, :], in_=pick[:, s, 0, :], func=COPY, scale=half_fk[:, a, t : t + 1])
+            for s in range(BATCH):
+                t = t0 + s
+                if group == last_group:
+                    nc.vector.scalar_tensor_tensor(
+                        out=flat[:, t, :], in0=pick[:, s, 1, :], scalar=fk_sb[:, a, t : t + 1], in1=both[:, s, 0, :],
+                        op0=ALU.mult, op1=ALU.add,
                     )
-                    pairs = psum.tile([P, 2, BLOCK], F32, name="pairs")
-                    words = rounded[:].bitcast(F32)
-                    for u in range(2):
-                        nc.tensor.transpose(pairs[:, u, :], words[:, u * P : (u + 1) * P], ident[:])
-                    nc.scalar.copy(
-                        out=grouped[:, b * BLOCK * PACK : (b + 1) * BLOCK * PACK].bitcast(F32).rearrange("p (j u) -> p j u", u=2),
-                        in_=pairs[:].rearrange("p u j -> p j u"),
+                else:
+                    nc.scalar.activation(out=both[:, s, 1, :], in_=pick[:, s, 1, :], func=COPY, scale=fk_sb[:, a, t : t + 1])
+            if group == last_group:
+                return
+            u = t0 // BATCH
+            for b0 in range(0, n // BLOCK, 2):
+                nb = min(2, n // BLOCK - b0)
+                sums = psum.tile([P, nb, BATCH, P], F32, name="sums", bufs=3)
+                terms = [(term, s, b) for term in range(2) for s in range(BATCH) for b in range(nb)]
+                for term, s, b in terms:
+                    cols = slice((b0 + b) * BLOCK, (b0 + b + 1) * BLOCK)
+                    nc.tensor.matmul(
+                        sums[:, b, s, :], lhsT=both[:, s, term, cols], rhs=ident[:], is_transpose=True,
+                        start=((term, s, b) == terms[0]), stop=((term, s, b) == terms[-1]),
                     )
-            codes = ring.tile([P, n], U32, name="codes", bufs=3, align_bytes=64)
-            plane = ring.tile([P, n], U8, name="plane", bufs=3, align_bytes=64)
-            nc.vector.quantize_mx(out=codes[:].bitcast(FP8X4), scales=plane[:], in_=grouped[:])
-            quantised[j0, a] = (codes, plane)
+                rounded = ring.tile([P, nb * P * BATCH], BF16, name="rounded")
+                nc.scalar.copy(
+                    out=rounded[:].rearrange("j (b p e) -> j b p e", b=nb, e=BATCH),
+                    in_=sums[:].rearrange("j b e p -> j b p e"),
+                )
+                if u == 0:
+                    pairs[group, b0] = psum.tile([P, nb, 2, BLOCK], F32, name="pairs")
+                words = rounded[:].bitcast(F32)
+                for b in range(nb):
+                    nc.tensor.transpose(pairs[group, b0][:, b, u, :], words[:, b * P : (b + 1) * P], ident[:])
 
-        def multiply(j0, b, a):
-            codes, plane = quantised[j0, a]
-            if a == 0:
-                accs[j0, b] = psum.tile([P, N], F32, name="acc")
-            cols = slice(b * BLOCK, (b + 1) * BLOCK)
-            nc.tensor.matmul_mx(
-                out=accs[j0, b][:], lhsT=codes[:, cols].bitcast(FP8X4), lhsT_scale=plane[:, cols],
-                rhs=w_codes[:, a, :].bitcast(FP8X4), rhs_scale=w_plane[:, a, :],
-                start=(a == 0), stop=(a == PASSES - 1),
+        def regroup(group):
+            j0, n, a = group
+            grouped[group] = held.tile([P, n * PACK], BF16, name="hold%d_%d_%d" % group, align_bytes=64)
+            for b0 in range(0, n // BLOCK, 2):
+                nb = min(2, n // BLOCK - b0)
+                words = grouped[group][:, b0 * BLOCK * PACK : (b0 + nb) * BLOCK * PACK].bitcast(F32)
+                nc.scalar.copy(
+                    out=words.rearrange("p (b j u) -> p b j u", b=nb, u=2),
+                    in_=pairs[group, b0][:].rearrange("p b u j -> p b j u"),
+                )
+
+        def quantise(group):
+            j0, n, a = group
+            codes = held.tile([P, n], U32, name="codes%d_%d_%d" % group, align_bytes=64)
+            plane = held.tile([P, n], U8, name="plane%d_%d_%d" % group, align_bytes=64)
+            nc.vector.quantize_mx(out=codes[:].bitcast(FP8X4), scales=plane[:], in_=grouped[group][:])
+            for b in range(n // BLOCK):
+                cols = slice(b * BLOCK, (b + 1) * BLOCK)
+                quantised[j0 // BLOCK + b, a] = (codes[:, cols], plane[:, cols])
+
+        def quantise_flat(b):
+            j0, n, a = last_group
+            block = (j0 + b * BLOCK, BLOCK, a)
+            grouped[block] = held.tile([P, BLOCK * PACK], BF16, name="last%d" % b, align_bytes=64)
+            nc.vector.tensor_copy(
+                out=grouped[block][:].rearrange("p (c i t) -> p c t i", i=4, t=PACK),
+                in_=flat[:, :, b * BLOCK : (b + 1) * BLOCK].rearrange("p t (c i) -> p c t i", i=4),
             )
+            return block
 
-        def hand_out(j0, b):
-            jb = j0 // BLOCK + b
+        def multiply(jb):
+            acc = psum.tile([P, N], F32, name="acc")
+            order = (1, 0) if jb < 2 else (0, 1)
+            for a in order:
+                codes, plane = quantised[jb, a]
+                nc.tensor.matmul_mx(
+                    out=acc[:], lhsT=codes.bitcast(FP8X4), lhsT_scale=plane,
+                    rhs=w_codes[:, a, :].bitcast(FP8X4), rhs_scale=w_plane[:, a, :],
+                    start=(a == order[0]), stop=(a == order[-1]),
+                )
+            return acc
+
+        def store_values(jb, y_sb):
+            nc.sync.dma_start(out=y_rows[:, :, jb * BLOCK : (jb + 1) * BLOCK], in_=y_sb[:])
+
+        def store_codes(jb, y_grouped):
             cols = slice(jb * BLOCK, (jb + 1) * BLOCK)
-            last = jb == J // BLOCK - 1
-            y_slots = ring.tile([P, PACK, P], F32, name="y_slots")
+            nc.vector.quantize_mx(out=y_codes[:, cols].bitcast(FP8X4), scales=y_plane[:, cols], in_=y_grouped[:])
+            nc.sync.dma_start(out=words_out[:, cols], in_=y_codes[:, cols].bitcast(I32))
+
+        def hand_out(jb):
+            acc = multiply(jb)
+            y_slots = held.tile([P, PACK, P], F32, name="y_slots%d" % jb)
             nc.scalar.activation(
-                out=y_slots[:], in_=accs[j0, b][:].rearrange("j (p t) -> j t p", t=PACK), func=COPY, scale=rw_sb[:, jb : jb + 1]
+                out=y_slots[:], in_=acc[:].rearrange("j (p t) -> j t p", t=PACK), func=COPY, scale=rw_sb[:, jb : jb + 1]
             )
             y_bank = psum.tile([P, PACK, BLOCK], F32, name="y_bank", bufs=1)
             for t in range(PACK):
                 nc.tensor.transpose(y_bank[:, t, :], y_slots[:, t, :], ident[:])
-            y_grouped = ring.tile([P, BLOCK * PACK], BF16, name="y_grouped", align_bytes=64)
-            grouped_view = y_grouped[:].rearrange("p (j t) -> p j t", t=PACK)
-            bank_view = y_bank[:].rearrange("p t j -> p j t")
-            if last:
-                nc.vector.tensor_copy(out=grouped_view, in_=bank_view)
-            else:
-                nc.scalar.copy(out=grouped_view, in_=bank_view)
+            y_grouped = held.tile([P, BLOCK * PACK], BF16, name="y_grouped%d" % jb, align_bytes=64)
+            nc.scalar.copy(out=y_grouped[:].rearrange("p (j t) -> p j t", t=PACK), in_=y_bank[:].rearrange("p t j -> p j t"))
             y_sb = ring.tile([P, PACK, BLOCK], F32, name="y_sb")
             nc.scalar.copy(out=y_sb[:], in_=y_bank[:])
-            nc.sync.dma_start(out=y_rows[:, :, cols], in_=y_sb[:])
-            nc.vector.quantize_mx(out=y_codes[:, cols].bitcast(FP8X4), scales=y_plane[:, cols], in_=y_grouped[:])
-            nc.sync.dma_start(out=words_out[:, cols], in_=y_codes[:, cols].bitcast(I32))
+            store_values(jb, y_sb)
+            waiting.append((jb, y_grouped))
 
-        def after(step):
-            j0, n, i = step
-            a, t = divmod(i, PACK)
-            if (j0, a) == last_group:
-                finish_on_vector(step)
-            if t != PACK - 1:
-                return
-            quantise(j0, n, a)
-            early = j0 > 0
-            for b in range(n // BLOCK):
-                if a == 0 and early:
-                    multiply(j0, b, 0)
-                if a == PASSES - 1:
-                    if not early:
-                        multiply(j0, b, 0)
-                    multiply(j0, b, 1)
-                    hand_out(j0, b)
+        def hand_out_last(jb):
+            acc = multiply(jb)
+            y_slots = ring.tile([P, PACK, P], F32, name="y_slots")
+            nc.vector.tensor_scalar(
+                out=y_slots[:], in0=acc[:].rearrange("j (p t) -> j t p", t=PACK), scalar1=rw_sb[:, jb : jb + 1],
+                scalar2=None, op0=ALU.mult,
+            )
+            banks = [psum.tile([P, 2, BLOCK], F32, name="pairs") for h in range(2)]
+            for t in range(PACK):
+                nc.tensor.transpose(banks[t // 2][:, t % 2, :], y_slots[:, t, :], ident[:])
+            y_sb = held.tile([P, PACK, BLOCK], F32, name="y_last")
+            nc.vector.tensor_copy(out=y_sb[:, 0:2, :], in_=banks[0][:])
+            nc.vector.tensor_copy(out=y_sb[:, 2:4, :], in_=banks[1][:])
+            y_grouped = ring.tile([P, BLOCK * PACK], BF16, name="y_grouped", align_bytes=64)
+            nc.vector.tensor_copy(
+                out=y_grouped[:].rearrange("p (c i t) -> p c t i", i=4, t=PACK),
+                in_=y_sb[:].rearrange("p t (c i) -> p c t i", i=4),
+            )
+            store_values(jb, y_sb)
+            store_codes(jb, y_grouped)
 
-        gather_first(steps[0])
-        for s in range(len(steps) + 2):
-            if s + 1 < len(steps):
-                gather_first(steps[s + 1])
-            if s < len(steps):
-                gather_others(steps[s])
-            if 1 <= s <= len(steps):
-                largest(steps[s - 1])
-            if s >= 2:
-                after(steps[s - 2])
+        flat = held.tile([P, PACK, last_group[1]], BF16, name="flat")
+        waiting = []
+        first, middle = GROUPS[:2]
+        for group in (first, middle):
+            for t0 in range(0, PACK, BATCH):
+                look_up(group, t0)
+            regroup(group)
+            if group == first:
+                quantise(first)
+        look_up(last_group, 0)
+        quantise(middle)
+        look_up(last_group, BATCH)
+        for jb in range(2):
+            hand_out(jb)
+            store_codes(*waiting.pop())
+        for block in [quantise_flat(b) for b in range(2)]:
+            quantise(block)
+        hand_out(2)
+        store_codes(*waiting.pop())
+        hand_out_last(3)
 
         for q in range(4):
             queue = nc.scalar if q % 2 else nc.sync

from contextlib import ExitStack

import concourse.mybir as mybir
from concourse.masks import make_identity

K, T, J, N = 1024, 1024, 512, 512
FLOPS = 2 * K * J * N

F32 = mybir.dt.float32
BF16 = mybir.dt.bfloat16
I32 = mybir.dt.int32
U32 = mybir.dt.uint32
U16 = mybir.dt.uint16
U8 = mybir.dt.uint8
FP8X4 = mybir.dt.float8_e4m3fn_x4
ALU = mybir.AluOpType
COPY = mybir.ActivationFunctionType.Copy

P = 128
PACK = 4
PASSES = K // (P * PACK)
BLOCK = 128
GROUPS = ((0, 512, 0), (0, 256, 1), (256, 256, 1))
BATCH = 2


def tile_list_largest_of_three_lists_pl_kernel(tc, xf, fk, w_words, w_scales, rw, offs, offs2, offs3, out_0, out_1, out_2):
    nc = tc.nc
    with ExitStack() as ctx:
        held = ctx.enter_context(tc.tile_pool(name="held", bufs=1))
        ring = ctx.enter_context(tc.tile_pool(name="ring", bufs=2))
        psum = ctx.enter_context(tc.psum_pool(name="psum", bufs=2))

        lists = [held.tile([P, J // 16], U16, name="list%d" % i) for i in range(3)]
        planes = [held.tile([P, T], F32, name="plane%d" % i) for i in range(PASSES * PACK)]
        fk_sb = held.tile([P, PASSES, PACK], F32)
        half_fk = held.tile([P, PASSES, PACK], F32)
        rw_sb = held.tile([P, J // BLOCK], F32)
        w_codes = held.tile([P, PASSES, N], U32, align_bytes=64)
        w_plane = held.tile([P, PASSES, N], U8, align_bytes=64)
        ident = held.tile([P, P], F32)
        y_codes = held.tile([P, J], U32, align_bytes=64)
        y_plane = held.tile([P, J], U8, align_bytes=64)

        x_rows = xf.rearrange("(a p t) c -> a t p c", a=PASSES, t=PACK)

        def load_plane(i):
            nc.sync.dma_start(out=planes[i][:], in_=x_rows[i // PACK, i % PACK])

        nc.gpsimd.memset(w_plane[:].rearrange("p a n -> p (a n)").bitcast(U32), 0)
        make_identity(nc, ident[:])

        nc.sync.dma_start(lists[0][:], offs)
        load_plane(0)
        nc.sync.dma_start(lists[1][:], offs2)
        nc.sync.dma_start(lists[2][:], offs3)
        nc.sync.dma_start(out=fk_sb[:], in_=fk.rearrange("(a p t) o -> p a (t o)", a=PASSES, t=PACK))
        for i in range(1, PASSES * PACK):
            load_plane(i)
        nc.sync.dma_start(
            out=w_codes[:].bitcast(I32),
            in_=w_words.rearrange("a p n r -> p a (n r)").bitcast(I32),
        )
        for q in range(4):
            nc.sync.dma_start(
                out=w_plane[32 * q : 32 * q + 4].bitcast(I32),
                in_=w_scales[:, 4 * q : 4 * q + 4, :].rearrange("a r n -> r a n").bitcast(I32),
            )
        with nc.allow_non_contiguous_dma(reason="one weight to a partition"):
            nc.sync.dma_start(out=rw_sb[:], in_=rw.rearrange("o (b p) -> p (o b)", p=BLOCK))
        nc.scalar.activation(out=half_fk[:], in_=fk_sb[:], func=COPY, scale=0.5)

        y_rows = out_0.rearrange("(p t) j -> p t j", t=PACK)
        words_out = out_1[0].rearrange("p j r -> p (j r)").bitcast(I32)

        last_group = GROUPS[-1]
        scaled = {}
        batches = [(group, t0) for group in GROUPS for t0 in range(0, PACK, BATCH)]
        pairs = {}
        grouped = {}
        quantised = {}

        def look_up(group, t0):
            j0, n, a = group

            def window(t, which):
                return planes[a * PACK + t][:].indirect(lists[which][:, j0 // 16 : (j0 + n) // 16])

            if (group, t0) == batches[-1]:
                pick = held.tile([P, BATCH, 2, n], F32, name="hold%d_%d_%d" % GROUPS[-2], align_bytes=64)
            else:
                pick = ring.tile([P, BATCH, 2, n], F32, name="pick", bufs=2)
            diff = ring.tile([P, BATCH, 2, n], F32, name="diff", bufs=2)
            for s in range(BATCH):
                nc.vector.tensor_copy(pick[:, s, 0, :], window(t0 + s, 0))
            for s in range(BATCH):
                for w in range(2):
                    nc.vector.tensor_tensor(diff[:, s, w, :], window(t0 + s, w + 1), pick[:, s, 0, :], ALU.subtract)
            for s in range(BATCH):
                nc.vector.scalar_tensor_tensor(
                    out=pick[:, s, 1, :], in0=diff[:, s, 0, :], scalar=0.0, in1=diff[:, s, 1, :], op0=ALU.max, op1=ALU.max
                )
            both = ring.tile([P, BATCH, 2, n], F32, name="both", bufs=3)
            for s in range(BATCH):
                t = t0 + s
                nc.scalar.activation(out=both[:, s, 0, :], in_=pick[:, s, 0, :], func=COPY, scale=half_fk[:, a, t : t + 1])
            for s in range(BATCH):
                t = t0 + s
                if group == last_group:
                    nc.vector.scalar_tensor_tensor(
                        out=flat[:, t, :], in0=pick[:, s, 1, :], scalar=fk_sb[:, a, t : t + 1], in1=both[:, s, 0, :],
                        op0=ALU.mult, op1=ALU.add,
                    )
                else:
                    nc.scalar.activation(out=both[:, s, 1, :], in_=pick[:, s, 1, :], func=COPY, scale=fk_sb[:, a, t : t + 1])
            if group == last_group:
                return
            u = t0 // BATCH
            for b0 in range(0, n // BLOCK, 2):
                nb = min(2, n // BLOCK - b0)
                sums = psum.tile([P, nb, BATCH, P], F32, name="sums", bufs=3)
                terms = [(term, s, b) for term in range(2) for s in range(BATCH) for b in range(nb)]
                for term, s, b in terms:
                    cols = slice((b0 + b) * BLOCK, (b0 + b + 1) * BLOCK)
                    nc.tensor.matmul(
                        sums[:, b, s, :], lhsT=both[:, s, term, cols], rhs=ident[:], is_transpose=True,
                        start=((term, s, b) == terms[0]), stop=((term, s, b) == terms[-1]),
                    )
                rounded = ring.tile([P, nb * P * BATCH], BF16, name="rounded")
                nc.scalar.copy(
                    out=rounded[:].rearrange("j (b p e) -> j b p e", b=nb, e=BATCH),
                    in_=sums[:].rearrange("j b e p -> j b p e"),
                )
                if u == 0:
                    pairs[group, b0] = psum.tile([P, nb, 2, BLOCK], F32, name="pairs")
                words = rounded[:].bitcast(F32)
                for b in range(nb):
                    nc.tensor.transpose(pairs[group, b0][:, b, u, :], words[:, b * P : (b + 1) * P], ident[:])

        def regroup(group):
            j0, n, a = group
            grouped[group] = held.tile([P, n * PACK], BF16, name="hold%d_%d_%d" % group, align_bytes=64)
            for b0 in range(0, n // BLOCK, 2):
                nb = min(2, n // BLOCK - b0)
                words = grouped[group][:, b0 * BLOCK * PACK : (b0 + nb) * BLOCK * PACK].bitcast(F32)
                nc.scalar.copy(
                    out=words.rearrange("p (b j u) -> p b j u", b=nb, u=2),
                    in_=pairs[group, b0][:].rearrange("p b u j -> p b j u"),
                )

        def quantise(group):
            j0, n, a = group
            codes = held.tile([P, n], U32, name="codes%d_%d_%d" % group, align_bytes=64)
            plane = held.tile([P, n], U8, name="plane%d_%d_%d" % group, align_bytes=64)
            nc.vector.quantize_mx(out=codes[:].bitcast(FP8X4), scales=plane[:], in_=grouped[group][:])
            for b in range(n // BLOCK):
                cols = slice(b * BLOCK, (b + 1) * BLOCK)
                quantised[j0 // BLOCK + b, a] = (codes[:, cols], plane[:, cols])

        def quantise_flat(b):
            j0, n, a = last_group
            block = (j0 + b * BLOCK, BLOCK, a)
            grouped[block] = held.tile([P, BLOCK * PACK], BF16, name="last%d" % b, align_bytes=64)
            nc.vector.tensor_copy(
                out=grouped[block][:].rearrange("p (c i t) -> p c t i", i=4, t=PACK),
                in_=flat[:, :, b * BLOCK : (b + 1) * BLOCK].rearrange("p t (c i) -> p c t i", i=4),
            )
            return block

        def multiply(jb):
            acc = psum.tile([P, N], F32, name="acc")
            order = (1, 0) if jb < 2 else (0, 1)
            for a in order:
                codes, plane = quantised[jb, a]
                nc.tensor.matmul_mx(
                    out=acc[:], lhsT=codes.bitcast(FP8X4), lhsT_scale=plane,
                    rhs=w_codes[:, a, :].bitcast(FP8X4), rhs_scale=w_plane[:, a, :],
                    start=(a == order[0]), stop=(a == order[-1]),
                )
            return acc

        def store_values(jb, y_sb):
            nc.sync.dma_start(out=y_rows[:, :, jb * BLOCK : (jb + 1) * BLOCK], in_=y_sb[:])

        def store_codes(jb, y_grouped):
            cols = slice(jb * BLOCK, (jb + 1) * BLOCK)
            nc.vector.quantize_mx(out=y_codes[:, cols].bitcast(FP8X4), scales=y_plane[:, cols], in_=y_grouped[:])
            nc.sync.dma_start(out=words_out[:, cols], in_=y_codes[:, cols].bitcast(I32))

        def hand_out(jb):
            acc = multiply(jb)
            y_slots = held.tile([P, PACK, P], F32, name="y_slots%d" % jb)
            nc.scalar.activation(
                out=y_slots[:], in_=acc[:].rearrange("j (p t) -> j t p", t=PACK), func=COPY, scale=rw_sb[:, jb : jb + 1]
            )
            y_bank = psum.tile([P, PACK, BLOCK], F32, name="y_bank", bufs=1)
            for t in range(PACK):
                nc.tensor.transpose(y_bank[:, t, :], y_slots[:, t, :], ident[:])
            y_grouped = held.tile([P, BLOCK * PACK], BF16, name="y_grouped%d" % jb, align_bytes=64)
            nc.scalar.copy(out=y_grouped[:].rearrange("p (j t) -> p j t", t=PACK), in_=y_bank[:].rearrange("p t j -> p j t"))
            y_sb = ring.tile([P, PACK, BLOCK], F32, name="y_sb")
            nc.scalar.copy(out=y_sb[:], in_=y_bank[:])
            store_values(jb, y_sb)
            waiting.append((jb, y_grouped))

        def hand_out_last(jb):
            acc = multiply(jb)
            y_slots = ring.tile([P, PACK, P], F32, name="y_slots")
            nc.vector.tensor_scalar(
                out=y_slots[:], in0=acc[:].rearrange("j (p t) -> j t p", t=PACK), scalar1=rw_sb[:, jb : jb + 1],
                scalar2=None, op0=ALU.mult,
            )
            banks = [psum.tile([P, 2, BLOCK], F32, name="pairs") for h in range(2)]
            for t in range(PACK):
                nc.tensor.transpose(banks[t // 2][:, t % 2, :], y_slots[:, t, :], ident[:])
            y_sb = held.tile([P, PACK, BLOCK], F32, name="y_last")
            nc.vector.tensor_copy(out=y_sb[:, 0:2, :], in_=banks[0][:])
            nc.vector.tensor_copy(out=y_sb[:, 2:4, :], in_=banks[1][:])
            y_grouped = ring.tile([P, BLOCK * PACK], BF16, name="y_grouped", align_bytes=64)
            nc.vector.tensor_copy(
                out=y_grouped[:].rearrange("p (c i t) -> p c t i", i=4, t=PACK),
                in_=y_sb[:].rearrange("p t (c i) -> p c t i", i=4),
            )
            store_values(jb, y_sb)
            store_codes(jb, y_grouped)

        flat = held.tile([P, PACK, last_group[1]], BF16, name="flat")
        waiting = []
        first, middle = GROUPS[:2]
        for group in (first, middle):
            for t0 in range(0, PACK, BATCH):
                look_up(group, t0)
            regroup(group)
            if group == first:
                quantise(first)
        look_up(last_group, 0)
        quantise(middle)
        look_up(last_group, BATCH)
        for jb in range(2):
            hand_out(jb)
            store_codes(*waiting.pop())
        for block in [quantise_flat(b) for b in range(2)]:
            quantise(block)
        hand_out(2)
        store_codes(*waiting.pop())
        hand_out_last(3)

        for q in range(4):
            queue = nc.scalar if q % 2 else nc.sync
            queue.dma_start(
                out=out_2[0, 4 * q : 4 * q + 4, :].bitcast(I32), in_=y_plane[32 * q : 32 * q + 4, :].bitcast(I32)
            )
